import numpy as np
import ml_dtypes

BF16 = ml_dtypes.bfloat16


def bf(x):
    return np.asarray(x, np.float32).astype(BF16)


def f32(x):
    return np.asarray(x, np.float32)


def f64(x):
    return np.asarray(x).astype(np.float64)


def striped(idx):
    return np.tile(idx.reshape(-1, 16).T, (8, 1))


def rows(idx, k):
    return np.tile(idx, (k, 1))


def look(tab, idx):
    return np.take_along_axis(f64(tab), rows(idx, len(tab)), axis=1)


K, S, V, N, M = 128, 2048, 2048, 2048, 512


def setup_inputs():
    return {"tab": f32(np.random.standard_normal((2, K, S))), "y": f32(np.random.standard_normal((K, V))), "w": bf(np.random.standard_normal((K, M)) / np.sqrt(K)), "b": f32(0.5 * np.random.standard_normal((M, 1))), "offs": striped(np.random.permutation(S)[:N])}


def reference(tab, y, w, b, offs):
    idx = offs[:16].T.reshape(-1)
    x = (np.minimum(look(tab[0], idx), f64(y))) * (1.0 / (1.0 + np.exp(-look(tab[1], idx))))
    return np.maximum(f64(w).T @ x + f64(b), 0.0)

@@ -1,0 +1,58 @@
+import concourse.mybir as mybir
+
+F32, BF16, U16 = mybir.dt.float32, mybir.dt.bfloat16, mybir.dt.uint16
+ALU, ACT = mybir.AluOpType, mybir.ActivationFunctionType
+
+P = 128
+S = 2048
+N = 2048
+M = 512
+BLOCKS = M // P
+PIECE = 512
+PSUM_BANKS = 8
+ENTRIES_PER_COLUMN = 16
+
+FLOPS = 2 * P * M * N
+
+
+def tile_lookup_vg_minsig_relu_kernel(tc, tab, y, w, b, offs, out):
+    nc = tc.nc
+    with (
+        tc.tile_pool(name="held", bufs=1) as held,
+        tc.tile_pool(name="work", bufs=N // PIECE) as work,
+        tc.psum_pool(name="psum", bufs=PSUM_BANKS) as psum,
+    ):
+        offsets = held.tile([P, N // ENTRIES_PER_COLUMN], U16)
+        gates = held.tile([P, S], F32)
+        values = held.tile([P, S], F32)
+        stream = held.tile([P, N], F32)
+        weights = held.tile([P, M], BF16)
+        bias = held.tile([P, BLOCKS], F32)
+
+        nc.sync.dma_start(offsets[:], offs)
+        nc.sync.dma_start(gates[:], tab[1])
+        nc.sync.dma_start(values[:], tab[0])
+        nc.sync.dma_start(stream[:, 0:PIECE], y[:, 0:PIECE])
+        nc.sync.dma_start(weights[:], w)
+        nc.sync.dma_start(bias[:], b.rearrange("(p k) one -> p (k one)", k=BLOCKS))
+        nc.sync.dma_start(stream[:, PIECE:N], y[:, PIECE:N])
+        out_blocks = out.rearrange("(p k) n -> k p n", k=BLOCKS)
+
+        for start in range(0, N, PIECE):
+            cols = slice(start, start + PIECE)
+            piece = offsets[:, start // ENTRIES_PER_COLUMN : (start + PIECE) // ENTRIES_PER_COLUMN]
+            gate = work.tile([P, PIECE], F32)
+            nc.scalar.activation(gate[:], gates[:].indirect(piece), ACT.Sigmoid)
+            low = work.tile([P, PIECE], F32)
+            nc.vector.tensor_tensor(low[:], values[:].indirect(piece), stream[:, cols], ALU.min)
+            x = work.tile([P, PIECE], BF16)
+            nc.vector.tensor_tensor(x[:], low[:], gate[:], ALU.mult)
+            for k in range(BLOCKS):
+                product = psum.tile([P, PIECE], F32)
+                nc.tensor.matmul(product[:], weights[:, k::BLOCKS], x[:], start=True, stop=True)
+                result = work.tile([P, PIECE], F32, tag=f"result{k}")
+                if k == BLOCKS - 1:
+                    nc.vector.tensor_scalar(result[:], product[:], bias[:, k : k + 1], 0.0, ALU.add, ALU.max)
+                else:
+                    nc.scalar.activation(result[:], product[:], ACT.Relu, bias=bias[:, k : k + 1])
+                nc.sync.dma_start(out_blocks[k][:, cols], result[:])

@@ -8,9 +8,12 @@ S = 2048
 N = 2048
 M = 512
 BLOCKS = M // P
-PIECE = 512
+BANK = 512
 PSUM_BANKS = 8
 ENTRIES_PER_COLUMN = 16
+STARTS = [0, BANK // 2, *range(BANK, N + 1, BANK)]
+PIECES = [slice(start, stop) for start, stop in zip(STARTS, STARTS[1:])]
+SHARED_PIECES = 2
 
 FLOPS = 2 * P * M * N
 
@@ -19,40 +22,60 @@ def tile_lookup_vg_minsig_relu_kernel(tc, tab, y, w, b, offs, out):
     nc = tc.nc
     with (
         tc.tile_pool(name="held", bufs=1) as held,
-        tc.tile_pool(name="work", bufs=N // PIECE) as work,
         tc.psum_pool(name="psum", bufs=PSUM_BANKS) as psum,
     ):
         offsets = held.tile([P, N // ENTRIES_PER_COLUMN], U16)
-        gates = held.tile([P, S], F32)
-        values = held.tile([P, S], F32)
+        gate_table = held.tile([P, S], F32)
+        value_table = held.tile([P, S], F32)
         stream = held.tile([P, N], F32)
         weights = held.tile([P, M], BF16)
         bias = held.tile([P, BLOCKS], F32)
+        gate = held.tile([P, N], F32)
+        low = held.tile([P, N], F32)
+        x = held.tile([P, N], BF16)
+        result = held.tile([P, BLOCKS, N], F32)
 
+        nc.sync.dma_start(gate_table[:], tab[1])
         nc.sync.dma_start(offsets[:], offs)
-        nc.sync.dma_start(gates[:], tab[1])
-        nc.sync.dma_start(values[:], tab[0])
-        nc.sync.dma_start(stream[:, 0:PIECE], y[:, 0:PIECE])
+        nc.sync.dma_start(value_table[:], tab[0])
+        nc.sync.dma_start(stream[:, PIECES[0]], y[:, PIECES[0]])
         nc.sync.dma_start(weights[:], w)
         nc.sync.dma_start(bias[:], b.rearrange("(p k) one -> p (k one)", k=BLOCKS))
-        nc.sync.dma_start(stream[:, PIECE:N], y[:, PIECE:N])
+        for cols in PIECES[1:]:
+            nc.sync.dma_start(stream[:, cols], y[:, cols])
         out_blocks = out.rearrange("(p k) n -> k p n", k=BLOCKS)
 
-        for start in range(0, N, PIECE):
-            cols = slice(start, start + PIECE)
-            piece = offsets[:, start // ENTRIES_PER_COLUMN : (start + PIECE) // ENTRIES_PER_COLUMN]
-            gate = work.tile([P, PIECE], F32)
-            nc.scalar.activation(gate[:], gates[:].indirect(piece), ACT.Sigmoid)
-            low = work.tile([P, PIECE], F32)
-            nc.vector.tensor_tensor(low[:], values[:].indirect(piece), stream[:, cols], ALU.min)
-            x = work.tile([P, PIECE], BF16)
-            nc.vector.tensor_tensor(x[:], low[:], gate[:], ALU.mult)
+        zero = held.tile([P, 1], F32)
+        warm = held.tile([P, 1], F32)
+        nc.vector.memset(zero[:], 0.0)
+        nc.scalar.activation(warm[:], zero[:], ACT.Sigmoid)
+
+        def listed(cols):
+            return offsets[:, cols.start // ENTRIES_PER_COLUMN : cols.stop // ENTRIES_PER_COLUMN]
+
+        def look_up_gates(cols):
+            nc.scalar.activation(gate[:, cols], gate_table[:].indirect(listed(cols)), ACT.Sigmoid)
+
+        def make_x(cols):
+            nc.vector.tensor_tensor(low[:, cols], value_table[:].indirect(listed(cols)), stream[:, cols], ALU.min)
+            nc.vector.tensor_tensor(x[:, cols], low[:, cols], gate[:, cols], ALU.mult)
+
+        def dense_layer(cols, vector_blocks):
             for k in range(BLOCKS):
-                product = psum.tile([P, PIECE], F32)
-                nc.tensor.matmul(product[:], weights[:, k::BLOCKS], x[:], start=True, stop=True)
-                result = work.tile([P, PIECE], F32, tag=f"result{k}")
-                if k == BLOCKS - 1:
-                    nc.vector.tensor_scalar(result[:], product[:], bias[:, k : k + 1], 0.0, ALU.add, ALU.max)
+                bank = psum.tile([P, BANK], F32)
+                product = bank[:, : cols.stop - cols.start]
+                nc.tensor.matmul(product, weights[:, k::BLOCKS], x[:, cols], start=True, stop=True)
+                if k in vector_blocks:
+                    nc.vector.tensor_scalar(result[:, k, cols], product, bias[:, k : k + 1], 0.0, ALU.add, ALU.max)
                 else:
-                    nc.scalar.activation(result[:], product[:], ACT.Relu, bias=bias[:, k : k + 1])
-                nc.sync.dma_start(out_blocks[k][:, cols], result[:])
+                    nc.scalar.activation(result[:, k, cols], product, ACT.Relu, bias=bias[:, k : k + 1])
+                nc.sync.dma_start(out_blocks[k][:, cols], result[:, k, cols])
+
+        for cols in PIECES:
+            look_up_gates(cols)
+        for cols in PIECES:
+            make_x(cols)
+        for cols in PIECES[:-SHARED_PIECES]:
+            dense_layer(cols, ())
+        for cols in PIECES[-SHARED_PIECES:]:
+            dense_layer(cols, (1, 3))

@@ -11,9 +11,8 @@ BLOCKS = M // P
 BANK = 512
 PSUM_BANKS = 8
 ENTRIES_PER_COLUMN = 16
-STARTS = [0, BANK // 2, *range(BANK, N + 1, BANK)]
+STARTS = [0, *range(BANK // 2, N - BANK, BANK), N]
 PIECES = [slice(start, stop) for start, stop in zip(STARTS, STARTS[1:])]
-SHARED_PIECES = 2
 
 FLOPS = 2 * P * M * N
 
@@ -60,22 +59,29 @@ def tile_lookup_vg_minsig_relu_kernel(tc, tab, y, w, b, offs, out):
             nc.vector.tensor_tensor(low[:, cols], value_table[:].indirect(listed(cols)), stream[:, cols], ALU.min)
             nc.vector.tensor_tensor(x[:, cols], low[:, cols], gate[:, cols], ALU.mult)
 
-        def dense_layer(cols, vector_blocks):
-            for k in range(BLOCKS):
-                bank = psum.tile([P, BANK], F32)
-                product = bank[:, : cols.stop - cols.start]
-                nc.tensor.matmul(product, weights[:, k::BLOCKS], x[:, cols], start=True, stop=True)
-                if k in vector_blocks:
-                    nc.vector.tensor_scalar(result[:, k, cols], product, bias[:, k : k + 1], 0.0, ALU.add, ALU.max)
-                else:
-                    nc.scalar.activation(result[:, k, cols], product, ACT.Relu, bias=bias[:, k : k + 1])
-                nc.sync.dma_start(out_blocks[k][:, cols], result[:, k, cols])
+        def product(k, cols):
+            bank = psum.tile([P, BANK], F32)
+            used = bank[:, : cols.stop - cols.start]
+            nc.tensor.matmul(used, weights[:, k::BLOCKS], x[:, cols], start=True, stop=True)
+            return used
 
-        for cols in PIECES:
-            look_up_gates(cols)
+        def finish_on_scalar(k, cols):
+            nc.scalar.activation(result[:, k, cols], product(k, cols), ACT.Relu, bias=bias[:, k : k + 1])
+
+        def finish_on_vector(k, cols):
+            nc.vector.tensor_scalar(result[:, k, cols], product(k, cols), bias[:, k : k + 1], 0.0, ALU.add, ALU.max)
+
+        look_up_gates(slice(0, N // 2))
+        look_up_gates(slice(N // 2, N))
         for cols in PIECES:
             make_x(cols)
-        for cols in PIECES[:-SHARED_PIECES]:
-            dense_layer(cols, ())
-        for cols in PIECES[-SHARED_PIECES:]:
-            dense_layer(cols, (1, 3))
+        for cols in PIECES[:-1]:
+            for k in range(BLOCKS):
+                finish_on_scalar(k, cols)
+                nc.sync.dma_start(out_blocks[k][:, cols], result[:, k, cols])
+        cols = PIECES[-1]
+        middle = (cols.start + cols.stop) // 2
+        for k in range(BLOCKS):
+            finish_on_vector(k, slice(cols.start, middle))
+            finish_on_scalar(k, slice(middle, cols.stop))
+            nc.sync.dma_start(out_blocks[k][:, cols], result[:, k, cols])

import concourse.mybir as mybir

F32, BF16, U16 = mybir.dt.float32, mybir.dt.bfloat16, mybir.dt.uint16
ALU, ACT = mybir.AluOpType, mybir.ActivationFunctionType

P = 128
S = 2048
N = 2048
M = 512
BLOCKS = M // P
BANK = 512
PSUM_BANKS = 8
ENTRIES_PER_COLUMN = 16
STARTS = [0, *range(BANK // 2, N - BANK, BANK), N]
PIECES = [slice(start, stop) for start, stop in zip(STARTS, STARTS[1:])]

FLOPS = 2 * P * M * N


def tile_lookup_vg_minsig_relu_kernel(tc, tab, y, w, b, offs, out):
    nc = tc.nc
    with (
        tc.tile_pool(name="held", bufs=1) as held,
        tc.psum_pool(name="psum", bufs=PSUM_BANKS) as psum,
    ):
        offsets = held.tile([P, N // ENTRIES_PER_COLUMN], U16)
        gate_table = held.tile([P, S], F32)
        value_table = held.tile([P, S], F32)
        stream = held.tile([P, N], F32)
        weights = held.tile([P, M], BF16)
        bias = held.tile([P, BLOCKS], F32)
        gate = held.tile([P, N], F32)
        low = held.tile([P, N], F32)
        x = held.tile([P, N], BF16)
        result = held.tile([P, BLOCKS, N], F32)

        nc.sync.dma_start(gate_table[:], tab[1])
        nc.sync.dma_start(offsets[:], offs)
        nc.sync.dma_start(value_table[:], tab[0])
        nc.sync.dma_start(stream[:, PIECES[0]], y[:, PIECES[0]])
        nc.sync.dma_start(weights[:], w)
        nc.sync.dma_start(bias[:], b.rearrange("(p k) one -> p (k one)", k=BLOCKS))
        for cols in PIECES[1:]:
            nc.sync.dma_start(stream[:, cols], y[:, cols])
        out_blocks = out.rearrange("(p k) n -> k p n", k=BLOCKS)

        zero = held.tile([P, 1], F32)
        warm = held.tile([P, 1], F32)
        nc.vector.memset(zero[:], 0.0)
        nc.scalar.activation(warm[:], zero[:], ACT.Sigmoid)

        def listed(cols):
            return offsets[:, cols.start // ENTRIES_PER_COLUMN : cols.stop // ENTRIES_PER_COLUMN]

        def look_up_gates(cols):
            nc.scalar.activation(gate[:, cols], gate_table[:].indirect(listed(cols)), ACT.Sigmoid)

        def make_x(cols):
            nc.vector.tensor_tensor(low[:, cols], value_table[:].indirect(listed(cols)), stream[:, cols], ALU.min)
            nc.vector.tensor_tensor(x[:, cols], low[:, cols], gate[:, cols], ALU.mult)

        def product(k, cols):
            bank = psum.tile([P, BANK], F32)
            used = bank[:, : cols.stop - cols.start]
            nc.tensor.matmul(used, weights[:, k::BLOCKS], x[:, cols], start=True, stop=True)
            return used

        def finish_on_scalar(k, cols):
            nc.scalar.activation(result[:, k, cols], product(k, cols), ACT.Relu, bias=bias[:, k : k + 1])

        def finish_on_vector(k, cols):
            nc.vector.tensor_scalar(result[:, k, cols], product(k, cols), bias[:, k : k + 1], 0.0, ALU.add, ALU.max)

        look_up_gates(slice(0, N // 2))
        look_up_gates(slice(N // 2, N))
        for cols in PIECES:
            make_x(cols)
        for cols in PIECES[:-1]:
            for k in range(BLOCKS):
                finish_on_scalar(k, cols)
                nc.sync.dma_start(out_blocks[k][:, cols], result[:, k, cols])
        cols = PIECES[-1]
        middle = (cols.start + cols.stop) // 2
        for k in range(BLOCKS):
            finish_on_vector(k, slice(cols.start, middle))
            finish_on_scalar(k, slice(middle, cols.stop))
            nc.sync.dma_start(out_blocks[k][:, cols], result[:, k, cols])
